import numpy as np
import ml_dtypes


def mxq(x, axis, fmt="e4m3"):
    dtype, down = {"e4m3": (ml_dtypes.float8_e4m3fn, 7), "e5m2": (ml_dtypes.float8_e5m2, 14)}[fmt]
    v = np.moveaxis(np.asarray(x, np.float32).astype(ml_dtypes.bfloat16).astype(np.float64), axis, -1)
    blocks = v.reshape(v.shape[:-1] + (-1, 32))
    amax = np.abs(blocks).max(-1, keepdims=True)
    byte = np.maximum(np.where(amax > 0, np.frexp(amax)[1] - 1 + 127, 0) - down, 1)
    scale = np.exp2(byte - 127.0)
    codes = (blocks / scale).astype(np.float32).astype(dtype).astype(np.float64)
    return np.moveaxis((codes * scale).reshape(v.shape), -1, axis)


WIDE = False


def mx_kscale(k):
    if not WIDE:
        return np.ones(k)
    levels = np.array([10, -10, 5, -5, 0])
    if k % 512:
        return np.exp2(np.random.permutation(np.resize(levels, k // 32))).repeat(32)
    a = np.empty((k // 512, 16))
    for p in range(k // 512):
        a[p, :8] = np.random.permutation(np.resize(levels, 8))
        for g in range(8):
            far = levels[np.abs(levels - a[p, g]) >= 10]
            a[p, g + 8] = far[np.random.randint(len(far))]
    return np.exp2(a.ravel()).repeat(32)


def f64(x):
    return np.asarray(x).astype(np.float64)


def striped(idx):
    return np.tile(np.asarray(idx).reshape(-1, 16).T, (8, 1)).astype(np.uint16)


def unstriped(offs):
    return offs[:16].T.reshape(-1).astype(np.int64)


E2M1 = np.array([0.0, 0.5, 1.0, 1.5, 2.0, 3.0, 4.0, 6.0, -0.0, -0.5, -1.0, -1.5, -2.0, -3.0, -4.0, -6.0])


def pack_weight(w, fmt):
    k, n = w.shape
    w = f64(np.asarray(w, np.float32).astype(ml_dtypes.bfloat16)).reshape(k // 32, 32, n)
    amax = np.abs(w).max(1)
    if fmt == "e4m3":
        byte = np.frexp(amax)[1] - 1 + 127 - 7
    else:
        mant, ex = np.frexp(amax / 6.0)
        byte = np.where(mant > 0.5, ex, ex - 1) + 127
    byte = np.clip(np.where(amax > 0, byte, 1), 1, 254)
    scaled = (w * np.exp2(127.0 - byte)[:, None, :]).reshape(k, n).astype(np.float32)
    by_word = np.ascontiguousarray(scaled.reshape(k // 512, 128, 4, n).transpose(0, 1, 3, 2))
    if fmt == "e4m3":
        words = by_word.astype(ml_dtypes.float8_e4m3fn).view(np.uint8)
    else:
        c = by_word.astype(ml_dtypes.float4_e2m1fn).view(np.uint8) & 0xF
        words = (c[..., 0::2] | (c[..., 1::2] << 4)).reshape(k // 512, 128, 2 * n)
    return np.ascontiguousarray(words), np.ascontiguousarray(byte.astype(np.uint8).reshape(k // 512, 16, n))


def unpack_weight(words, scales, fmt):
    g, _, n = scales.shape
    words = np.ascontiguousarray(words).reshape(g, 128, n, -1)
    if fmt == "e4m3":
        vals = words.view(ml_dtypes.float8_e4m3fn).astype(np.float64)
    else:
        nib = np.empty((g, 128, n, 4), np.uint8)
        nib[..., 0::2] = words & 0xF
        nib[..., 1::2] = words >> 4
        vals = E2M1[nib]
    vals = vals * np.repeat(np.exp2(scales.astype(np.float64) - 127.0), 8, axis=1)[..., None]
    return vals.transpose(0, 1, 3, 2).reshape(g * 512, n)


def bf(x):
    return np.asarray(x, np.float32).astype(ml_dtypes.bfloat16)


def planes(Y):
    r, m = Y.shape
    b = f64(bf(Y)).reshape(r // 32, 32, m)
    amax = np.abs(b).max(1)
    byte = np.clip(np.where(amax > 0, np.frexp(amax)[1] - 1 + 127 - 7, 1), 1, 254)
    codes = (b * np.exp2(127.0 - byte)[:, None, :]).reshape(r, m).astype(np.float32).astype(ml_dtypes.float8_e4m3fn).view(np.uint8)
    words = codes.reshape(r // 512, 128, 4, m).transpose(0, 1, 3, 2)
    return np.ascontiguousarray(words), np.ascontiguousarray(byte.astype(np.uint8).reshape(r // 512, 16, m))


D, T, I, J, U, E = 512, 2048, 512, 512, 1024, 512


def setup_inputs():
    n = np.random.standard_normal
    idx = np.random.permutation(T)[:I]
    idx2 = np.random.permutation(U)[:J]
    idx3 = np.random.permutation(U)[:J]
    fd = mx_kscale(D)
    fi = mx_kscale(I)
    ti = np.ones(T)
    ti[idx] = fi
    keysp = pack_weight(n((D, T)) / fd[:, None], "e2m1")
    return {
        "keys_words": keysp[0],
        "keys_scales": keysp[1],
        "notes": (n((D, U)) * 1.0 / np.sqrt(D) * fd[:, None]).astype(np.float32),
        "rowf": (np.random.uniform(0.02, 0.08, (I, 1)) * fi[:, None]).astype(np.float32),
        "vals": (n((E, T)) / ti).astype(np.float32),
        "offs": striped(idx),
        "offs2": striped(idx2),
        "offs3": striped(idx3),
    }


def reference(keys_words, keys_scales, notes, rowf, vals, offs, offs2, offs3):
    idx = unstriped(offs)
    idx2 = unstriped(offs2)
    idx3 = unstriped(offs3)
    keysu = unpack_weight(keys_words, keys_scales, "e2m1")
    keysidxg = keysu[:, idx]
    notesq = mxq(f64(notes), 0, "e4m3")
    g1 = keysidxg.T @ notesq
    g9 = g1[:, idx2] - g1[:, idx3]
    g0 = np.maximum(g9, 0.0)
    gr1 = g0 * f64(rowf)
    vt1 = f64(vals)[:, idx].T
    vt1q = mxq(vt1, 0, "e4m3")
    gr1q = mxq(gr1, 0, "e4m3")
    o = vt1q.T @ gr1q
    words, scales = planes(o)
    return o, words, scales

@@ -1,0 +1,222 @@
+from contextlib import ExitStack
+
+import concourse.mybir as mybir
+from concourse.masks import make_identity
+
+D, T, I, J, U, E = 512, 2048, 512, 512, 1024, 512
+FLOPS = 2 * D * I * U + 2 * I * E * J
+
+F32 = mybir.dt.float32
+BF16 = mybir.dt.bfloat16
+I32 = mybir.dt.int32
+U32 = mybir.dt.uint32
+U16 = mybir.dt.uint16
+U8 = mybir.dt.uint8
+FP8X4 = mybir.dt.float8_e4m3fn_x4
+FP4X4 = mybir.dt.float4_e2m1fn_x4
+ALU = mybir.AluOpType
+COPY = mybir.ActivationFunctionType.Copy
+
+P = 128
+PACK = 4
+RUN = 4
+BANK = 512
+NOTE_CHUNKS = ((0, 512), (512, 256), (768, 256))
+
+
+def interleave(copy, grouped, planes):
+    copy(
+        out=grouped.rearrange("p (c i) t -> p c t i", i=RUN),
+        in_=planes.rearrange("p t (c i) -> p c t i", i=RUN),
+    )
+
+
+def quantise(nc, codes, scales, grouped):
+    nc.vector.quantize_mx(out=codes.bitcast(FP8X4), scales=scales, in_=grouped.rearrange("p c t -> p (c t)"))
+
+
+def tile_attend_tab_looked_exchange_pl_kernel(
+    tc, keys_words, keys_scales, notes, rowf, vals, offs, offs2, offs3, out_0, out_1, out_2
+):
+    nc = tc.nc
+    with ExitStack() as ctx:
+        lists = ctx.enter_context(tc.tile_pool(name="lists", bufs=1))
+        sb = ctx.enter_context(tc.tile_pool(name="sb", bufs=1))
+        psum = ctx.enter_context(tc.psum_pool(name="psum", bufs=1))
+
+        idx = lists.tile([P, I // 16], U16, name="idx")
+        idx2 = lists.tile([P, J // 16], U16, name="idx2")
+        idx3 = lists.tile([P, J // 16], U16, name="idx3")
+
+        key_words = sb.tile([P, T], U16, name="key_words", align_bytes=64)
+        key_scales = sb.tile([P, T], U8, name="key_scales", align_bytes=64)
+        nc.vector.memset(key_scales[:].bitcast(I32), 0)
+        nc.sync.dma_start(idx[:], offs)
+        for q in range(4):
+            nc.scalar.dma_start(
+                key_scales[32 * q : 32 * q + 4, :].bitcast(I32), keys_scales[0, 4 * q : 4 * q + 4, :].bitcast(I32)
+            )
+        nc.sync.dma_start(idx3[:], offs3)
+        nc.sync.dma_start(idx2[:], offs2)
+        factor = sb.tile([P, PACK], F32, name="factor")
+        nc.sync.dma_start(factor[:], rowf.rearrange("(p t) o -> p (t o)", t=PACK))
+        nc.sync.dma_start(key_words[:].bitcast(I32), keys_words[0].bitcast(I32))
+
+        notes_rows = notes.rearrange("(p t) u -> p t u", t=PACK)
+        notes_raw = []
+        for n, (u0, width) in enumerate(NOTE_CHUNKS):
+            raw = sb.tile([P, PACK, width], F32, name="notes_raw%d" % n)
+            nc.sync.dma_start(raw[:], notes_rows[:, :, u0 : u0 + width])
+            notes_raw.append(raw)
+        vals_rows = vals.rearrange("(p r) c -> p r c", r=PACK)
+        vals_plane = []
+        for r in range(PACK):
+            plane = sb.tile([P, T], F32, name="vals_plane%d" % r)
+            nc.sync.dma_start(plane[:], vals_rows[:, r, :])
+            vals_plane.append(plane)
+
+        identity = sb.tile([P, P], F32, name="identity")
+        make_identity(nc, identity[:])
+
+        picked_scales = sb.tile([P, I], U8, name="picked_scales", align_bytes=64)
+        picked_words = sb.tile([P, I], U16, name="picked_words", align_bytes=64)
+        dealt_words = sb.tile([P, I], U16, name="dealt_words", align_bytes=64)
+        nc.vector.tensor_copy(picked_words[:], key_words[:].indirect(idx[:]))
+        nc.vector.tensor_copy(
+            picked_scales[:].rearrange("p (t s) -> p s t", t=PACK), key_scales[:].indirect(idx[:])
+        )
+        nc.vector.tensor_copy(
+            dealt_words[:].rearrange("p (t s) -> p t s", t=PACK),
+            picked_words[:].rearrange("p (s t) -> p t s", t=PACK),
+        )
+
+        notes_grouped = sb.tile([P, U, PACK], BF16, name="notes_grouped", align_bytes=64)
+        notes_codes = sb.tile([P, U], U32, name="notes_codes", align_bytes=64)
+        notes_scales = sb.tile([P, U], U8, name="notes_scales", align_bytes=64)
+
+        def quantise_notes(n):
+            u0, width = NOTE_CHUNKS[n]
+            cols = slice(u0, u0 + width)
+            quantise(nc, notes_codes[:, cols], notes_scales[:, cols], notes_grouped[:, cols, :])
+
+        def score(bank, t, n):
+            u0, width = NOTE_CHUNKS[n]
+            cols = slice(u0, u0 + width)
+            rows = slice(t * P, (t + 1) * P)
+            nc.tensor.matmul_mx(
+                out=bank[:, u0 % BANK : u0 % BANK + width],
+                lhsT=dealt_words[:, rows].bitcast(FP4X4),
+                lhsT_scale=picked_scales[:, rows],
+                rhs=notes_codes[:, cols].bitcast(FP8X4),
+                rhs_scale=notes_scales[:, cols],
+                start=True,
+                stop=True,
+            )
+
+        wide = [sb.tile([P, U], F32, name="wide%d" % t) for t in range(PACK)]
+
+        interleave(nc.scalar.copy, notes_grouped[:, 256:512, :], notes_raw[0][:, :, 256:512])
+        interleave(nc.vector.tensor_copy, notes_grouped[:, 0:256, :], notes_raw[0][:, :, 0:256])
+        quantise_notes(0)
+        left_banks = []
+        for t in range(PACK):
+            bank = psum.tile([P, BANK], F32, name="left%d" % t, tag="acc", bufs=6)
+            score(bank, t, 0)
+            left_banks.append(bank)
+        interleave(nc.scalar.copy, notes_grouped[:, 512:768, :], notes_raw[1][:])
+        quantise_notes(1)
+        interleave(nc.vector.tensor_copy, notes_grouped[:, 768:1024, :], notes_raw[2][:])
+        quantise_notes(2)
+        for t in range(PACK):
+            nc.scalar.copy(out=wide[t][:, 0:BANK], in_=left_banks[t][:])
+        for t in range(PACK):
+            bank = psum.tile([P, BANK], F32, name="right%d" % t, tag="acc", bufs=6)
+            score(bank, t, 1)
+            score(bank, t, 2)
+            nc.vector.tensor_copy(out=wide[t][:, BANK:U], in_=bank[:])
+
+        vals_codes = sb.tile([P, E], U32, name="vals_codes", align_bytes=64)
+        vals_scales = sb.tile([P, E], U8, name="vals_scales", align_bytes=64)
+        vals_grouped = sb.tile([P, E, PACK], BF16, name="vals_grouped", align_bytes=64)
+        picked_vals = [sb.tile([P, I], BF16, name="picked_vals%d" % r) for r in range(PACK)]
+
+        def gather_vals(r):
+            nc.scalar.activation(picked_vals[r][:], vals_plane[r][:].indirect(idx[:]), COPY)
+
+        def turn_vals(r):
+            pairs = picked_vals[r][:].bitcast(F32)
+            turned = psum.tile([P, 2, P], F32, name="turned%d" % r, tag="turned", bufs=2)
+            for h in range(2):
+                nc.tensor.transpose(turned[:, h, :], pairs[:, h : I // 2 : 2], identity[:])
+            cols = slice(r * P, (r + 1) * P)
+            nc.scalar.copy(
+                out=vals_grouped[:, cols, :].bitcast(F32), in_=turned[:].rearrange("p h e -> p e h")
+            )
+
+        def quantise_vals(r):
+            cols = slice(r * P, (r + 1) * P)
+            quantise(nc, vals_codes[:, cols], vals_scales[:, cols], vals_grouped[:, cols, :])
+
+        second = [sb.tile([P, J], F32, name="second%d" % t) for t in range(PACK)]
+        diff = [sb.tile([P, J], F32, name="diff%d" % t) for t in range(PACK)]
+        table = sb.tile([P, PACK, J], BF16, name="table")
+        table_grouped = sb.tile([P, J, PACK], BF16, name="table_grouped", align_bytes=64)
+        table_codes = sb.tile([P, J], U32, name="table_codes", align_bytes=64)
+        table_scales = sb.tile([P, J], U8, name="table_scales", align_bytes=64)
+
+        def weigh(t):
+            nc.vector.tensor_scalar(table[:, t, :], diff[t][:], 0.0, factor[:, t : t + 1], ALU.max, ALU.mult)
+
+        for t in range(PACK):
+            nc.scalar.activation(second[t][:], wide[t][:].indirect(idx3[:]), COPY)
+            nc.vector.tensor_tensor(diff[t][:], wide[t][:].indirect(idx2[:]), second[t][:], ALU.subtract)
+            if t > 0:
+                weigh(t - 1)
+        gather_vals(0)
+        gather_vals(1)
+        turn_vals(0)
+        gather_vals(2)
+        turn_vals(1)
+        quantise_vals(0)
+        weigh(PACK - 1)
+        gather_vals(3)
+        turn_vals(2)
+        quantise_vals(1)
+        interleave(nc.vector.tensor_copy, table_grouped[:], table[:])
+        turn_vals(3)
+        quantise_vals(2)
+        quantise(nc, table_codes[:], table_scales[:], table_grouped[:])
+        quantise_vals(3)
+
+        result = sb.tile([P, PACK, J], F32, name="result")
+        out_rows = out_0.rearrange("(p r) j -> p r j", r=PACK)
+        for r in range(PACK):
+            cols = slice(r * P, (r + 1) * P)
+            bank = psum.tile([P, BANK], F32, name="sum%d" % r, tag="acc", bufs=6)
+            nc.tensor.matmul_mx(
+                out=bank[:],
+                lhsT=vals_codes[:, cols].bitcast(FP8X4),
+                lhsT_scale=vals_scales[:, cols],
+                rhs=table_codes[:].bitcast(FP8X4),
+                rhs_scale=table_scales[:],
+                start=True,
+                stop=True,
+            )
+            if r % 2 == 0:
+                nc.scalar.copy(out=result[:, r, :], in_=bank[:])
+            else:
+                nc.vector.tensor_copy(out=result[:, r, :], in_=bank[:])
+            nc.sync.dma_start(out_rows[:, r, :], result[:, r, :])
+
+        result_grouped = sb.tile([P, J, PACK], BF16, name="result_grouped", align_bytes=64)
+        result_codes = sb.tile([P, J], U32, name="result_codes", align_bytes=64)
+        result_scales = sb.tile([P, J], U8, name="result_scales", align_bytes=64)
+        out_words = out_1[0].rearrange("p c r -> p (c r)").bitcast(I32)
+        interleave(nc.scalar.copy, result_grouped[:, 384:512, :], result[:, :, 384:512])
+        interleave(nc.vector.tensor_copy, result_grouped[:, 0:384, :], result[:, :, 0:384])
+        quantise(nc, result_codes[:], result_scales[:], result_grouped[:])
+        nc.sync.dma_start(out_words, result_codes[:].bitcast(I32))
+        for q in range(4):
+            nc.scalar.dma_start(
+                out_2[0, 4 * q : 4 * q + 4, :].bitcast(I32), result_scales[32 * q : 32 * q + 4, :].bitcast(I32)
+            )

@@ -21,7 +21,10 @@ P = 128
 PACK = 4
 RUN = 4
 BANK = 512
-NOTE_CHUNKS = ((0, 512), (512, 256), (768, 256))
+NOTE_CHUNKS = ((0, 512), (512, 512))
+LEFT_SPLIT = 256
+RIGHT_SPLIT = 384
+TAIL_SPLIT = 384
 
 
 def interleave(copy, grouped, planes):
@@ -51,27 +54,27 @@ def tile_attend_tab_looked_exchange_pl_kernel(
         key_words = sb.tile([P, T], U16, name="key_words", align_bytes=64)
         key_scales = sb.tile([P, T], U8, name="key_scales", align_bytes=64)
         nc.vector.memset(key_scales[:].bitcast(I32), 0)
+        nc.sync.dma_start(key_words[:].bitcast(I32), keys_words[0].bitcast(I32))
         nc.sync.dma_start(idx[:], offs)
+        nc.sync.dma_start(idx3[:], offs3)
         for q in range(4):
-            nc.scalar.dma_start(
+            nc.sync.dma_start(
                 key_scales[32 * q : 32 * q + 4, :].bitcast(I32), keys_scales[0, 4 * q : 4 * q + 4, :].bitcast(I32)
             )
-        nc.sync.dma_start(idx3[:], offs3)
-        nc.sync.dma_start(idx2[:], offs2)
-        factor = sb.tile([P, PACK], F32, name="factor")
-        nc.sync.dma_start(factor[:], rowf.rearrange("(p t) o -> p (t o)", t=PACK))
-        nc.sync.dma_start(key_words[:].bitcast(I32), keys_words[0].bitcast(I32))
 
         notes_rows = notes.rearrange("(p t) u -> p t u", t=PACK)
         notes_raw = []
         for n, (u0, width) in enumerate(NOTE_CHUNKS):
-            raw = sb.tile([P, PACK, width], F32, name="notes_raw%d" % n)
+            raw = sb.tile([P, PACK, width], F32, name="notes_raw%d" % n, tag="raw%d" % n)
             nc.sync.dma_start(raw[:], notes_rows[:, :, u0 : u0 + width])
             notes_raw.append(raw)
+        nc.sync.dma_start(idx2[:], offs2)
+        factor = sb.tile([P, PACK], F32, name="factor")
+        nc.sync.dma_start(factor[:], rowf.rearrange("(p t) o -> p (t o)", t=PACK))
         vals_rows = vals.rearrange("(p r) c -> p r c", r=PACK)
         vals_plane = []
         for r in range(PACK):
-            plane = sb.tile([P, T], F32, name="vals_plane%d" % r)
+            plane = sb.tile([P, T], F32, name="vals_plane%d" % r, tag="plane%d" % r, align_bytes=64)
             nc.sync.dma_start(plane[:], vals_rows[:, r, :])
             vals_plane.append(plane)
 
@@ -90,14 +93,14 @@ def tile_attend_tab_looked_exchange_pl_kernel(
             picked_words[:].rearrange("p (s t) -> p t s", t=PACK),
         )
 
-        notes_grouped = sb.tile([P, U, PACK], BF16, name="notes_grouped", align_bytes=64)
+        notes_grouped = sb.tile([P, BANK, PACK], BF16, name="notes_grouped", align_bytes=64)
         notes_codes = sb.tile([P, U], U32, name="notes_codes", align_bytes=64)
         notes_scales = sb.tile([P, U], U8, name="notes_scales", align_bytes=64)
 
         def quantise_notes(n):
             u0, width = NOTE_CHUNKS[n]
             cols = slice(u0, u0 + width)
-            quantise(nc, notes_codes[:, cols], notes_scales[:, cols], notes_grouped[:, cols, :])
+            quantise(nc, notes_codes[:, cols], notes_scales[:, cols], notes_grouped[:])
 
         def score(bank, t, n):
             u0, width = NOTE_CHUNKS[n]
@@ -113,51 +116,48 @@ def tile_attend_tab_looked_exchange_pl_kernel(
                 stop=True,
             )
 
-        wide = [sb.tile([P, U], F32, name="wide%d" % t) for t in range(PACK)]
+        wide = [sb.tile([P, U], F32, name="wide%d" % t, tag="raw1" if t == 0 else "wide%d" % t) for t in range(PACK)]
 
-        interleave(nc.scalar.copy, notes_grouped[:, 256:512, :], notes_raw[0][:, :, 256:512])
-        interleave(nc.vector.tensor_copy, notes_grouped[:, 0:256, :], notes_raw[0][:, :, 0:256])
-        quantise_notes(0)
-        left_banks = []
-        for t in range(PACK):
-            bank = psum.tile([P, BANK], F32, name="left%d" % t, tag="acc", bufs=6)
-            score(bank, t, 0)
-            left_banks.append(bank)
-        interleave(nc.scalar.copy, notes_grouped[:, 512:768, :], notes_raw[1][:])
-        quantise_notes(1)
-        interleave(nc.vector.tensor_copy, notes_grouped[:, 768:1024, :], notes_raw[2][:])
-        quantise_notes(2)
-        for t in range(PACK):
-            nc.scalar.copy(out=wide[t][:, 0:BANK], in_=left_banks[t][:])
-        for t in range(PACK):
-            bank = psum.tile([P, BANK], F32, name="right%d" % t, tag="acc", bufs=6)
-            score(bank, t, 1)
-            score(bank, t, 2)
-            nc.vector.tensor_copy(out=wide[t][:, BANK:U], in_=bank[:])
+        def round_notes(n, split):
+            u0, width = NOTE_CHUNKS[n]
+            interleave(nc.scalar.copy, notes_grouped[:, split:width, :], notes_raw[n][:, :, split:width])
+            interleave(nc.vector.tensor_copy, notes_grouped[:, 0:split, :], notes_raw[n][:, :, 0:split])
+            quantise_notes(n)
+
+        def score_half(t, n, copy):
+            bank = psum.tile([P, BANK], F32, name="score%d_%d" % (t, n), tag="acc", bufs=6)
+            score(bank, t, n)
+            copy(out=wide[t][:, n * BANK : (n + 1) * BANK], in_=bank[:])
+
+        round_notes(0, LEFT_SPLIT)
+        round_notes(1, RIGHT_SPLIT)
+        for t, n in ((0, 0), (1, 0), (2, 0), (3, 0), (0, 1), (1, 1), (2, 1), (3, 1)):
+            score_half(t, n, nc.scalar.copy if n == 0 and t < 3 else nc.vector.tensor_copy)
 
         vals_codes = sb.tile([P, E], U32, name="vals_codes", align_bytes=64)
         vals_scales = sb.tile([P, E], U8, name="vals_scales", align_bytes=64)
-        vals_grouped = sb.tile([P, E, PACK], BF16, name="vals_grouped", align_bytes=64)
-        picked_vals = [sb.tile([P, I], BF16, name="picked_vals%d" % r) for r in range(PACK)]
 
         def gather_vals(r):
             nc.scalar.activation(picked_vals[r][:], vals_plane[r][:].indirect(idx[:]), COPY)
 
-        def turn_vals(r):
-            pairs = picked_vals[r][:].bitcast(F32)
-            turned = psum.tile([P, 2, P], F32, name="turned%d" % r, tag="turned", bufs=2)
-            for h in range(2):
-                nc.tensor.transpose(turned[:, h, :], pairs[:, h : I // 2 : 2], identity[:])
-            cols = slice(r * P, (r + 1) * P)
+        def turn_vals(pair):
+            turned = psum.tile([P, 2, 2, P], F32, name="turned%d" % pair, tag="turned", bufs=2)
+            for s in range(2):
+                words = picked_vals[2 * pair + s][:].bitcast(F32)
+                for h in range(2):
+                    nc.tensor.transpose(turned[:, s, h, :], words[:, h : I // 2 : 2], identity[:])
+            cols = slice(2 * pair * P, (2 * pair + 2) * P)
             nc.scalar.copy(
-                out=vals_grouped[:, cols, :].bitcast(F32), in_=turned[:].rearrange("p h e -> p e h")
+                out=vals_grouped[:, cols, :].bitcast(F32).rearrange("p (s e) h -> p s e h", s=2),
+                in_=turned[:].rearrange("p s h e -> p s e h"),
             )
 
-        def quantise_vals(r):
-            cols = slice(r * P, (r + 1) * P)
-            quantise(nc, vals_codes[:, cols], vals_scales[:, cols], vals_grouped[:, cols, :])
-
-        second = [sb.tile([P, J], F32, name="second%d" % t) for t in range(PACK)]
+        picked_vals = [sb.tile([P, I], BF16, name="picked_vals0")]
+        gather_vals(0)
+        second = [
+            sb.tile([P, J], F32, name="second%d" % t, tag="plane%d" % t if t == 0 else "looked%d" % t, align_bytes=64)
+            for t in range(PACK)
+        ]
         diff = [sb.tile([P, J], F32, name="diff%d" % t) for t in range(PACK)]
         table = sb.tile([P, PACK, J], BF16, name="table")
         table_grouped = sb.tile([P, J, PACK], BF16, name="table_grouped", align_bytes=64)
@@ -172,51 +172,63 @@ def tile_attend_tab_looked_exchange_pl_kernel(
             nc.vector.tensor_tensor(diff[t][:], wide[t][:].indirect(idx2[:]), second[t][:], ALU.subtract)
             if t > 0:
                 weigh(t - 1)
-        gather_vals(0)
-        gather_vals(1)
-        turn_vals(0)
-        gather_vals(2)
-        turn_vals(1)
-        quantise_vals(0)
         weigh(PACK - 1)
-        gather_vals(3)
-        turn_vals(2)
-        quantise_vals(1)
         interleave(nc.vector.tensor_copy, table_grouped[:], table[:])
-        turn_vals(3)
-        quantise_vals(2)
+        for r in range(1, PACK):
+            tag = "plane0" if r == 1 else "looked%d" % (r - 1)
+            picked_vals.append(sb.tile([P, I], BF16, name="picked_vals%d" % r, tag=tag, align_bytes=64))
+            gather_vals(r)
+        vals_grouped = sb.tile([P, E, PACK], BF16, name="vals_grouped", tag="plane3", align_bytes=64)
+        for pair in range(2):
+            turn_vals(pair)
         quantise(nc, table_codes[:], table_scales[:], table_grouped[:])
-        quantise_vals(3)
+        for pair in range(2):
+            cols = slice(2 * pair * P, (2 * pair + 2) * P)
+            quantise(nc, vals_codes[:, cols], vals_scales[:, cols], vals_grouped[:, cols, :])
 
         result = sb.tile([P, PACK, J], F32, name="result")
         out_rows = out_0.rearrange("(p r) j -> p r j", r=PACK)
-        for r in range(PACK):
-            cols = slice(r * P, (r + 1) * P)
-            bank = psum.tile([P, BANK], F32, name="sum%d" % r, tag="acc", bufs=6)
-            nc.tensor.matmul_mx(
-                out=bank[:],
-                lhsT=vals_codes[:, cols].bitcast(FP8X4),
-                lhsT_scale=vals_scales[:, cols],
-                rhs=table_codes[:].bitcast(FP8X4),
-                rhs_scale=table_scales[:],
-                start=True,
-                stop=True,
-            )
-            if r % 2 == 0:
-                nc.scalar.copy(out=result[:, r, :], in_=bank[:])
-            else:
-                nc.vector.tensor_copy(out=result[:, r, :], in_=bank[:])
-            nc.sync.dma_start(out_rows[:, r, :], result[:, r, :])
-
         result_grouped = sb.tile([P, J, PACK], BF16, name="result_grouped", align_bytes=64)
         result_codes = sb.tile([P, J], U32, name="result_codes", align_bytes=64)
         result_scales = sb.tile([P, J], U8, name="result_scales", align_bytes=64)
         out_words = out_1[0].rearrange("p c r -> p (c r)").bitcast(I32)
-        interleave(nc.scalar.copy, result_grouped[:, 384:512, :], result[:, :, 384:512])
-        interleave(nc.vector.tensor_copy, result_grouped[:, 0:384, :], result[:, :, 0:384])
-        quantise(nc, result_codes[:], result_scales[:], result_grouped[:])
-        nc.sync.dma_start(out_words, result_codes[:].bitcast(I32))
+
+        def multiply(out, r, cols):
+            features = slice(r * P, (r + 1) * P)
+            nc.tensor.matmul_mx(
+                out=out,
+                lhsT=vals_codes[:, features].bitcast(FP8X4),
+                lhsT_scale=vals_scales[:, features],
+                rhs=table_codes[:, cols].bitcast(FP8X4),
+                rhs_scale=table_scales[:, cols],
+                start=True,
+                stop=True,
+            )
+
+        for r in range(2):
+            bank = psum.tile([P, J], F32, name="sum%d" % r, tag="acc", bufs=6)
+            multiply(bank[:], r, slice(0, J))
+            nc.scalar.copy(out=result[:, r, :], in_=bank[:])
+            nc.sync.dma_start(out_rows[:, r, :], result[:, r, :])
+        halves = (slice(0, J // 2), slice(J // 2, J))
+        for half, copy in zip(halves, (nc.vector.tensor_copy, nc.scalar.copy)):
+            bank = psum.tile([P, 2, J // 2], F32, name="sum_half", tag="acc", bufs=6)
+            for s in range(2):
+                multiply(bank[:, s, :], 2 + s, half)
+            copy(out=result[:, 2:4, half], in_=bank[:])
+            nc.sync.dma_start(out_rows[:, 2:4, half], result[:, 2:4, half])
+
+        def hand_on(half):
+            quantise(nc, result_codes[:, half], result_scales[:, half], result_grouped[:, half, :])
+            nc.sync.dma_start(out_words[:, half], result_codes[:, half].bitcast(I32))
+
+        interleave(nc.vector.tensor_copy, result_grouped[:, halves[0], :], result[:, :, halves[0]])
+        hand_on(halves[0])
+        interleave(nc.vector.tensor_copy, result_grouped[:, 256:TAIL_SPLIT, :], result[:, :, 256:TAIL_SPLIT])
+        interleave(nc.scalar.copy, result_grouped[:, TAIL_SPLIT:J, :], result[:, :, TAIL_SPLIT:J])
+        hand_on(halves[1])
         for q in range(4):
-            nc.scalar.dma_start(
+            queue = nc.scalar if q % 2 == 0 else nc.sync
+            queue.dma_start(
                 out_2[0, 4 * q : 4 * q + 4, :].bitcast(I32), result_scales[32 * q : 32 * q + 4, :].bitcast(I32)
             )

from contextlib import ExitStack

import concourse.mybir as mybir
from concourse.masks import make_identity

D, T, I, J, U, E = 512, 2048, 512, 512, 1024, 512
FLOPS = 2 * D * I * U + 2 * I * E * J

F32 = mybir.dt.float32
BF16 = mybir.dt.bfloat16
I32 = mybir.dt.int32
U32 = mybir.dt.uint32
U16 = mybir.dt.uint16
U8 = mybir.dt.uint8
FP8X4 = mybir.dt.float8_e4m3fn_x4
FP4X4 = mybir.dt.float4_e2m1fn_x4
ALU = mybir.AluOpType
COPY = mybir.ActivationFunctionType.Copy

P = 128
PACK = 4
RUN = 4
BANK = 512
NOTE_CHUNKS = ((0, 512), (512, 512))
LEFT_SPLIT = 256
RIGHT_SPLIT = 384
TAIL_SPLIT = 384


def interleave(copy, grouped, planes):
    copy(
        out=grouped.rearrange("p (c i) t -> p c t i", i=RUN),
        in_=planes.rearrange("p t (c i) -> p c t i", i=RUN),
    )


def quantise(nc, codes, scales, grouped):
    nc.vector.quantize_mx(out=codes.bitcast(FP8X4), scales=scales, in_=grouped.rearrange("p c t -> p (c t)"))


def tile_attend_tab_looked_exchange_pl_kernel(
    tc, keys_words, keys_scales, notes, rowf, vals, offs, offs2, offs3, out_0, out_1, out_2
):
    nc = tc.nc
    with ExitStack() as ctx:
        lists = ctx.enter_context(tc.tile_pool(name="lists", bufs=1))
        sb = ctx.enter_context(tc.tile_pool(name="sb", bufs=1))
        psum = ctx.enter_context(tc.psum_pool(name="psum", bufs=1))

        idx = lists.tile([P, I // 16], U16, name="idx")
        idx2 = lists.tile([P, J // 16], U16, name="idx2")
        idx3 = lists.tile([P, J // 16], U16, name="idx3")

        key_words = sb.tile([P, T], U16, name="key_words", align_bytes=64)
        key_scales = sb.tile([P, T], U8, name="key_scales", align_bytes=64)
        nc.vector.memset(key_scales[:].bitcast(I32), 0)
        nc.sync.dma_start(key_words[:].bitcast(I32), keys_words[0].bitcast(I32))
        nc.sync.dma_start(idx[:], offs)
        nc.sync.dma_start(idx3[:], offs3)
        for q in range(4):
            nc.sync.dma_start(
                key_scales[32 * q : 32 * q + 4, :].bitcast(I32), keys_scales[0, 4 * q : 4 * q + 4, :].bitcast(I32)
            )

        notes_rows = notes.rearrange("(p t) u -> p t u", t=PACK)
        notes_raw = []
        for n, (u0, width) in enumerate(NOTE_CHUNKS):
            raw = sb.tile([P, PACK, width], F32, name="notes_raw%d" % n, tag="raw%d" % n)
            nc.sync.dma_start(raw[:], notes_rows[:, :, u0 : u0 + width])
            notes_raw.append(raw)
        nc.sync.dma_start(idx2[:], offs2)
        factor = sb.tile([P, PACK], F32, name="factor")
        nc.sync.dma_start(factor[:], rowf.rearrange("(p t) o -> p (t o)", t=PACK))
        vals_rows = vals.rearrange("(p r) c -> p r c", r=PACK)
        vals_plane = []
        for r in range(PACK):
            plane = sb.tile([P, T], F32, name="vals_plane%d" % r, tag="plane%d" % r, align_bytes=64)
            nc.sync.dma_start(plane[:], vals_rows[:, r, :])
            vals_plane.append(plane)

        identity = sb.tile([P, P], F32, name="identity")
        make_identity(nc, identity[:])

        picked_scales = sb.tile([P, I], U8, name="picked_scales", align_bytes=64)
        picked_words = sb.tile([P, I], U16, name="picked_words", align_bytes=64)
        dealt_words = sb.tile([P, I], U16, name="dealt_words", align_bytes=64)
        nc.vector.tensor_copy(picked_words[:], key_words[:].indirect(idx[:]))
        nc.vector.tensor_copy(
            picked_scales[:].rearrange("p (t s) -> p s t", t=PACK), key_scales[:].indirect(idx[:])
        )
        nc.vector.tensor_copy(
            dealt_words[:].rearrange("p (t s) -> p t s", t=PACK),
            picked_words[:].rearrange("p (s t) -> p t s", t=PACK),
        )

        notes_grouped = sb.tile([P, BANK, PACK], BF16, name="notes_grouped", align_bytes=64)
        notes_codes = sb.tile([P, U], U32, name="notes_codes", align_bytes=64)
        notes_scales = sb.tile([P, U], U8, name="notes_scales", align_bytes=64)

        def quantise_notes(n):
            u0, width = NOTE_CHUNKS[n]
            cols = slice(u0, u0 + width)
            quantise(nc, notes_codes[:, cols], notes_scales[:, cols], notes_grouped[:])

        def score(bank, t, n):
            u0, width = NOTE_CHUNKS[n]
            cols = slice(u0, u0 + width)
            rows = slice(t * P, (t + 1) * P)
            nc.tensor.matmul_mx(
                out=bank[:, u0 % BANK : u0 % BANK + width],
                lhsT=dealt_words[:, rows].bitcast(FP4X4),
                lhsT_scale=picked_scales[:, rows],
                rhs=notes_codes[:, cols].bitcast(FP8X4),
                rhs_scale=notes_scales[:, cols],
                start=True,
                stop=True,
            )

        wide = [sb.tile([P, U], F32, name="wide%d" % t, tag="raw1" if t == 0 else "wide%d" % t) for t in range(PACK)]

        def round_notes(n, split):
            u0, width = NOTE_CHUNKS[n]
            interleave(nc.scalar.copy, notes_grouped[:, split:width, :], notes_raw[n][:, :, split:width])
            interleave(nc.vector.tensor_copy, notes_grouped[:, 0:split, :], notes_raw[n][:, :, 0:split])
            quantise_notes(n)

        def score_half(t, n, copy):
            bank = psum.tile([P, BANK], F32, name="score%d_%d" % (t, n), tag="acc", bufs=6)
            score(bank, t, n)
            copy(out=wide[t][:, n * BANK : (n + 1) * BANK], in_=bank[:])

        round_notes(0, LEFT_SPLIT)
        round_notes(1, RIGHT_SPLIT)
        for t, n in ((0, 0), (1, 0), (2, 0), (3, 0), (0, 1), (1, 1), (2, 1), (3, 1)):
            score_half(t, n, nc.scalar.copy if n == 0 and t < 3 else nc.vector.tensor_copy)

        vals_codes = sb.tile([P, E], U32, name="vals_codes", align_bytes=64)
        vals_scales = sb.tile([P, E], U8, name="vals_scales", align_bytes=64)

        def gather_vals(r):
            nc.scalar.activation(picked_vals[r][:], vals_plane[r][:].indirect(idx[:]), COPY)

        def turn_vals(pair):
            turned = psum.tile([P, 2, 2, P], F32, name="turned%d" % pair, tag="turned", bufs=2)
            for s in range(2):
                words = picked_vals[2 * pair + s][:].bitcast(F32)
                for h in range(2):
                    nc.tensor.transpose(turned[:, s, h, :], words[:, h : I // 2 : 2], identity[:])
            cols = slice(2 * pair * P, (2 * pair + 2) * P)
            nc.scalar.copy(
                out=vals_grouped[:, cols, :].bitcast(F32).rearrange("p (s e) h -> p s e h", s=2),
                in_=turned[:].rearrange("p s h e -> p s e h"),
            )

        picked_vals = [sb.tile([P, I], BF16, name="picked_vals0")]
        gather_vals(0)
        second = [
            sb.tile([P, J], F32, name="second%d" % t, tag="plane%d" % t if t == 0 else "looked%d" % t, align_bytes=64)
            for t in range(PACK)
        ]
        diff = [sb.tile([P, J], F32, name="diff%d" % t) for t in range(PACK)]
        table = sb.tile([P, PACK, J], BF16, name="table")
        table_grouped = sb.tile([P, J, PACK], BF16, name="table_grouped", align_bytes=64)
        table_codes = sb.tile([P, J], U32, name="table_codes", align_bytes=64)
        table_scales = sb.tile([P, J], U8, name="table_scales", align_bytes=64)

        def weigh(t):
            nc.vector.tensor_scalar(table[:, t, :], diff[t][:], 0.0, factor[:, t : t + 1], ALU.max, ALU.mult)

        for t in range(PACK):
            nc.scalar.activation(second[t][:], wide[t][:].indirect(idx3[:]), COPY)
            nc.vector.tensor_tensor(diff[t][:], wide[t][:].indirect(idx2[:]), second[t][:], ALU.subtract)
            if t > 0:
                weigh(t - 1)
        weigh(PACK - 1)
        interleave(nc.vector.tensor_copy, table_grouped[:], table[:])
        for r in range(1, PACK):
            tag = "plane0" if r == 1 else "looked%d" % (r - 1)
            picked_vals.append(sb.tile([P, I], BF16, name="picked_vals%d" % r, tag=tag, align_bytes=64))
            gather_vals(r)
        vals_grouped = sb.tile([P, E, PACK], BF16, name="vals_grouped", tag="plane3", align_bytes=64)
        for pair in range(2):
            turn_vals(pair)
        quantise(nc, table_codes[:], table_scales[:], table_grouped[:])
        for pair in range(2):
            cols = slice(2 * pair * P, (2 * pair + 2) * P)
            quantise(nc, vals_codes[:, cols], vals_scales[:, cols], vals_grouped[:, cols, :])

        result = sb.tile([P, PACK, J], F32, name="result")
        out_rows = out_0.rearrange("(p r) j -> p r j", r=PACK)
        result_grouped = sb.tile([P, J, PACK], BF16, name="result_grouped", align_bytes=64)
        result_codes = sb.tile([P, J], U32, name="result_codes", align_bytes=64)
        result_scales = sb.tile([P, J], U8, name="result_scales", align_bytes=64)
        out_words = out_1[0].rearrange("p c r -> p (c r)").bitcast(I32)

        def multiply(out, r, cols):
            features = slice(r * P, (r + 1) * P)
            nc.tensor.matmul_mx(
                out=out,
                lhsT=vals_codes[:, features].bitcast(FP8X4),
                lhsT_scale=vals_scales[:, features],
                rhs=table_codes[:, cols].bitcast(FP8X4),
                rhs_scale=table_scales[:, cols],
                start=True,
                stop=True,
            )

        for r in range(2):
            bank = psum.tile([P, J], F32, name="sum%d" % r, tag="acc", bufs=6)
            multiply(bank[:], r, slice(0, J))
            nc.scalar.copy(out=result[:, r, :], in_=bank[:])
            nc.sync.dma_start(out_rows[:, r, :], result[:, r, :])
        halves = (slice(0, J // 2), slice(J // 2, J))
        for half, copy in zip(halves, (nc.vector.tensor_copy, nc.scalar.copy)):
            bank = psum.tile([P, 2, J // 2], F32, name="sum_half", tag="acc", bufs=6)
            for s in range(2):
                multiply(bank[:, s, :], 2 + s, half)
            copy(out=result[:, 2:4, half], in_=bank[:])
            nc.sync.dma_start(out_rows[:, 2:4, half], result[:, 2:4, half])

        def hand_on(half):
            quantise(nc, result_codes[:, half], result_scales[:, half], result_grouped[:, half, :])
            nc.sync.dma_start(out_words[:, half], result_codes[:, half].bitcast(I32))

        interleave(nc.vector.tensor_copy, result_grouped[:, halves[0], :], result[:, :, halves[0]])
        hand_on(halves[0])
        interleave(nc.vector.tensor_copy, result_grouped[:, 256:TAIL_SPLIT, :], result[:, :, 256:TAIL_SPLIT])
        interleave(nc.scalar.copy, result_grouped[:, TAIL_SPLIT:J, :], result[:, :, TAIL_SPLIT:J])
        hand_on(halves[1])
        for q in range(4):
            queue = nc.scalar if q % 2 == 0 else nc.sync
            queue.dma_start(
                out_2[0, 4 * q : 4 * q + 4, :].bitcast(I32), result_scales[32 * q : 32 * q + 4, :].bitcast(I32)
            )
